import numpy as np
import ml_dtypes


def mxq(x, axis, fmt="e4m3"):
    dtype, down = {"e4m3": (ml_dtypes.float8_e4m3fn, 7), "e5m2": (ml_dtypes.float8_e5m2, 14)}[fmt]
    v = np.moveaxis(np.asarray(x, np.float32).astype(ml_dtypes.bfloat16).astype(np.float64), axis, -1)
    blocks = v.reshape(v.shape[:-1] + (-1, 32))
    amax = np.abs(blocks).max(-1, keepdims=True)
    byte = np.maximum(np.where(amax > 0, np.frexp(amax)[1] - 1 + 127, 0) - down, 1)
    scale = np.exp2(byte - 127.0)
    codes = (blocks / scale).astype(np.float32).astype(dtype).astype(np.float64)
    return np.moveaxis((codes * scale).reshape(v.shape), -1, axis)


WIDE = False


def mx_kscale(k):
    if not WIDE:
        return np.ones(k)
    levels = np.array([10, -10, 5, -5, 0])
    if k % 512:
        return np.exp2(np.random.permutation(np.resize(levels, k // 32))).repeat(32)
    a = np.empty((k // 512, 16))
    for p in range(k // 512):
        a[p, :8] = np.random.permutation(np.resize(levels, 8))
        for g in range(8):
            far = levels[np.abs(levels - a[p, g]) >= 10]
            a[p, g + 8] = far[np.random.randint(len(far))]
    return np.exp2(a.ravel()).repeat(32)


def f64(x):
    return np.asarray(x).astype(np.float64)


def striped(idx):
    return np.tile(idx.reshape(-1, 16).T, (8, 1)).astype(np.uint16)


def unstriped(offs):
    return offs[:16].T.reshape(-1).astype(np.int64)


def striped8(idx):
    return np.concatenate([x.reshape(-1, 16).T for x in idx]).astype(np.uint16)


def runs(offs, k):
    lists = np.stack([offs[16 * r : 16 * r + 16].T.reshape(-1) for r in range(8)]).astype(np.int64)
    return lists[np.arange(k) % 512 // 64]


def pack_weight(w):
    k, n = w.shape
    w = f64(np.asarray(w, np.float32).astype(ml_dtypes.bfloat16)).reshape(k // 32, 32, n)
    amax = np.abs(w).max(1)
    byte = np.clip(np.where(amax > 0, np.frexp(amax)[1] - 1 + 127 - 7, 1), 1, 254)
    scaled = (w * np.exp2(127.0 - byte)[:, None, :]).reshape(k, n).astype(np.float32)
    words = np.ascontiguousarray(scaled.reshape(k // 512, 128, 4, n).transpose(0, 1, 3, 2)).astype(ml_dtypes.float8_e4m3fn).view(np.uint8)
    return words, np.ascontiguousarray(byte.astype(np.uint8).reshape(k // 512, 16, n))


def unpack_weight(words, scales):
    g, p, n, _ = words.shape
    vals = np.ascontiguousarray(words).view(ml_dtypes.float8_e4m3fn).astype(np.float64) * np.repeat(np.exp2(scales.astype(np.float64) - 127.0), 8, axis=1)[..., None]
    return vals.transpose(0, 1, 3, 2).reshape(g * 512, n)


def sigmoid(v):
    return 1.0 / (1.0 + np.exp(-np.maximum(v, -700.0)))

def planes(y):
    n, m = y.shape
    v = y.astype(np.float32).astype(ml_dtypes.bfloat16).astype(np.float64).reshape(n // 32, 32, m)
    top = np.abs(v).max(1)
    byte = np.clip(np.where(top > 0, np.frexp(top)[1] - 1 + 127 - 7, 1), 1, 254)
    codes = (v * np.exp2(127.0 - byte)[:, None, :]).reshape(n, m).astype(np.float32).astype(ml_dtypes.float8_e4m3fn).view(np.uint8)
    words = codes.reshape(n // 512, 128, 4, m).transpose(0, 1, 3, 2)
    return np.ascontiguousarray(words), np.ascontiguousarray(byte.astype(np.uint8).reshape(n // 512, 16, m))


K, T, S, N, H, U = 512, 2048, 512, 512, 512, 1024


def setup_inputs():
    n = np.random.standard_normal
    s = mx_kscale(K)[:, None]
    u = mx_kscale(S)
    packed_xT = pack_weight(n((K, T)) * s)
    return {
        "x_words": packed_xT[0],
        "x_scales": packed_xT[1],
        "wa": (n((K, H)) / np.sqrt(K) / s).astype(np.float32),
        "wb": (n((K, N)) / np.sqrt(K) / s).astype(np.float32),
        "tau": np.random.uniform(0.3, 0.9, (S, 1)).astype(np.float32),
        "gt": (np.random.uniform(0.5, 1.5, (S, 1)) * u[:, None]).astype(np.float32),
        "gi": (np.random.uniform(0.5, 1.5, (S, 1)) / u[:, None]).astype(np.float32),
        "mem": n((H, U)).astype(np.float32),
        "sl": np.random.uniform(1.0, 2.0, (H, 1)).astype(np.float32),
        "th": (0.5 * n((H, 1))).astype(np.float32),
        "offs": striped(np.random.permutation(T)[:S]),
        "two": striped(np.random.permutation(T)[:S]),
        "n1": striped8(np.stack([np.random.permutation(H) for _ in range(8)])),
        "n2": striped(np.random.permutation(U)[:N]),
        "n3": striped(np.random.permutation(N)),
    }


def reference(x_words, x_scales, wa, wb, tau, gt, gi, mem, sl, th, offs, two, n1, n2, n3):
    old = f64(mem)[:, unstriped(n2)]
    xq = unpack_weight(x_words, x_scales)[:, unstriped(offs)]
    a = xq.T @ mxq(f64(wa), 0, "e4m3")
    top = a.max(axis=1, keepdims=True)
    own = np.exp(f64(tau) * (a - top))
    ea = np.exp(f64(tau) * (a[np.arange(S)[:, None], runs(n1, S)] - top))
    z = f64(gt) * ((2.0 * (a * own)) / (own + ea + 0.25))
    x_two = unpack_weight(x_words, x_scales)[:, unstriped(two)]
    b = x_two.T @ mxq(f64(wb), 0, "e4m3")
    z2 = f64(gi) * b
    cv = 0.0625 * ((mxq(z, 0, "e4m3").T @ mxq(z2, 0, "e4m3")))
    sg = sigmoid(f64(sl) * (cv[:, unstriped(n3)] - f64(th)))
    nw = old + sg * (cv - old)
    out = f64(mem).copy()
    out[:, unstriped(n2)] = nw
    return (out,) + planes(out)

@@ -1,0 +1,238 @@
+from contextlib import ExitStack
+
+import concourse.mybir as mybir
+
+F32 = mybir.dt.float32
+BF16 = mybir.dt.bfloat16
+I32 = mybir.dt.int32
+U32 = mybir.dt.uint32
+U16 = mybir.dt.uint16
+U8 = mybir.dt.uint8
+FP8X4 = mybir.dt.float8_e4m3fn_x4
+ALU = mybir.AluOpType
+ACT = mybir.ActivationFunctionType
+
+P = 128
+PACK = 4
+T = 2048
+S = 512
+U = 1024
+HALF = 256
+FLOPS = 3 * 2 * 512 * 512 * 512
+
+
+def tile_picked_momeshepg_none_po_kernel(
+    tc, x_words, x_scales, wa, wb, tau, gt, gi, mem, sl, th, offs, two, n1, n2, n3, out_0, out_1, out_2
+):
+    nc = tc.nc
+    with ExitStack() as ctx:
+        lists = ctx.enter_context(tc.tile_pool(name="lists", bufs=1))
+        keep = ctx.enter_context(tc.tile_pool(name="keep", bufs=1))
+        psum = ctx.enter_context(tc.psum_pool(name="psum", bufs=1))
+
+        def load_list(src, name):
+            tile = lists.tile([P, S // 16], U16, name=name)
+            nc.sync.dma_start(tile[:], src)
+            return tile
+
+        def load_rows(src, name):
+            tile = keep.tile([P, PACK], F32, name=name)
+            nc.sync.dma_start(tile[:], src.rearrange("(p t) o -> p (t o)", t=PACK))
+            return tile
+
+        def weave(engine_copy, dst, src):
+            engine_copy(
+                out=dst.rearrange("p (c i) j -> p c j i", i=4),
+                in_=src.rearrange("p j (c i) -> p c j i", i=4),
+            )
+
+        def quantize(src, width, name):
+            words = keep.tile([P, width], U32, name=name + "_words", align_bytes=64)
+            scales = keep.tile([P, width], U8, name=name + "_scales", align_bytes=64)
+            nc.vector.quantize_mx(out=words[:].bitcast(FP8X4), scales=scales[:], in_=src.rearrange("p w j -> p (w j)"))
+            return words, scales
+
+        x_scale_table = keep.tile([P, T], U8, name="x_scale_table")
+        nc.vector.memset(x_scale_table[:].bitcast(I32), 0)
+        offs_t = load_list(offs, "offs_t")
+        two_t = load_list(two, "two_t")
+        for q in range(4):
+            nc.sync.dma_start(x_scale_table[32 * q : 32 * q + 4, :].bitcast(I32), x_scales[0][4 * q : 4 * q + 4, :].bitcast(I32))
+        x_word_table = keep.tile([P, T], U32, name="x_word_table")
+        nc.sync.dma_start(x_word_table[:].bitcast(I32), x_words[0].rearrange("p c r -> p (c r)").bitcast(I32))
+        wa_rows = wa.rearrange("(p j) n -> p j n", j=PACK)
+        wa_raw = []
+        for h in range(2):
+            raw = keep.tile([P, PACK, HALF], F32, name=f"wa_raw{h}")
+            nc.sync.dma_start(raw[:], wa_rows[:, :, h * HALF : (h + 1) * HALF])
+            wa_raw.append(raw)
+        mem_rows = mem.rearrange("(p t) c -> t p c", t=PACK)
+        page = [keep.tile([P, U], F32, name=f"page{t}") for t in range(PACK)]
+        n2_t = load_list(n2, "n2_t")
+        n1_t = load_list(n1, "n1_t")
+        tau_t = load_rows(tau, "tau_t")
+        nc.sync.dma_start(page[0][:], mem_rows[0])
+        wb_raw = keep.tile([P, PACK, S], F32, name="wb_raw")
+        nc.sync.dma_start(wb_raw[:], wb.rearrange("(p j) n -> p j n", j=PACK))
+        gi_t = load_rows(gi, "gi_t")
+        gt_t = load_rows(gt, "gt_t")
+        for t in range(1, PACK):
+            nc.sync.dma_start(page[t][:], mem_rows[t])
+        n3_t = load_list(n3, "n3_t")
+        sl_t = load_rows(sl, "sl_t")
+        th_t = load_rows(th, "th_t")
+
+        def pick(table, entries, dtype, name):
+            picked = keep.tile([P, PACK, P], dtype, name=name, align_bytes=64)
+            nc.vector.tensor_copy(picked[:].rearrange("p t m -> p m t"), table[:].indirect(entries[:]))
+            return picked
+
+        xa_scales = pick(x_scale_table, offs_t, U8, "xa_scales")
+        xb_scales = pick(x_scale_table, two_t, U8, "xb_scales")
+        xa_words = pick(x_word_table, offs_t, U32, "xa_words")
+        xb_words = pick(x_word_table, two_t, U32, "xb_words")
+
+        a_bank = [psum.tile([P, S], F32, name=f"a_bank{t}") for t in range(PACK)]
+        wa_q = []
+        for h in range(2):
+            woven = keep.tile([P, HALF, PACK], BF16, name=f"wa_woven{h}", align_bytes=64)
+            weave(nc.scalar.copy, woven[:], wa_raw[h][:])
+            wa_q.append(quantize(woven[:], HALF, f"wa{h}"))
+        for h in range(2):
+            for t in range(PACK):
+                nc.tensor.matmul_mx(
+                    out=a_bank[t][:, h * HALF : (h + 1) * HALF],
+                    lhsT=xa_words[:, t, :].bitcast(FP8X4), lhsT_scale=xa_scales[:, t, :],
+                    rhs=wa_q[h][0][:].bitcast(FP8X4), rhs_scale=wa_q[h][1][:],
+                    start=True, stop=True,
+                )
+        ea = keep.tile([P, PACK, S], F32, name="ea")
+        shift = []
+        for t in range(PACK):
+            a_row = keep.tile([P, S], F32, name=f"a_row{t}")
+            top = keep.tile([P, 1], F32, name=f"top{t}")
+            nc.vector.tensor_scalar(a_row[:], a_bank[t][:], 1.0, None, ALU.mult, ALU.max, accum_out=top[:])
+            bias = keep.tile([P, 1], F32, name=f"shift{t}")
+            nc.gpsimd.tensor_scalar(bias[:], top[:], tau_t[:, t : t + 1], -1.0, ALU.mult, ALU.mult)
+            shift.append(bias)
+            for h in range(2):
+                nc.scalar.activation(
+                    ea[:, t, h * HALF : (h + 1) * HALF], a_row[:].indirect(n1_t[:, 16 * h : 16 * h + 16]), ACT.Exp,
+                    bias=bias[:], scale=tau_t[:, t : t + 1],
+                )
+
+        old0 = keep.tile([P, S], F32, name="old0")
+        nc.scalar.activation(old0[:], page[0][:].indirect(n2_t[:]), ACT.Copy)
+
+        wb_woven = keep.tile([P, S, PACK], BF16, name="wb_woven", align_bytes=64)
+        weave(nc.vector.tensor_copy, wb_woven[:], wb_raw[:])
+        wb_words, wb_scales = quantize(wb_woven[:], S, "wb")
+        z2 = keep.tile([P, S, PACK], BF16, name="z2", align_bytes=64)
+        for c in range(4):
+            b_bank = psum.tile([P, PACK, P], F32, name=f"b_bank{c}", tag=f"late{c}")
+            for t in range(PACK):
+                nc.tensor.matmul_mx(
+                    out=b_bank[:, t, :],
+                    lhsT=xb_words[:, t, :].bitcast(FP8X4), lhsT_scale=xb_scales[:, t, :],
+                    rhs=wb_words[:, c * P : (c + 1) * P].bitcast(FP8X4), rhs_scale=wb_scales[:, c * P : (c + 1) * P],
+                    start=True, stop=True,
+                )
+            nc.vector.tensor_tensor(
+                z2[:, c * P : (c + 1) * P, :], b_bank[:].rearrange("p t n -> p n t"),
+                gi_t[:].unsqueeze(1).to_broadcast([P, P, PACK]), ALU.mult,
+            )
+        z2_words, z2_scales = quantize(z2[:], S, "z2")
+
+        gt2 = keep.tile([P, PACK], F32, name="gt2")
+        nc.vector.tensor_scalar(gt2[:], gt_t[:], 2.0, None, ALU.mult)
+        sg_bias = keep.tile([P, PACK], F32, name="sg_bias")
+        nc.vector.scalar_tensor_tensor(sg_bias[:], sl_t[:], -1.0, th_t[:], ALU.mult, ALU.mult)
+        log_rest = keep.tile([P, PACK, S], F32, name="log_rest")
+        logit = keep.tile([P, PACK, S], F32, name="logit", tag="logit_then_old")
+        for h in range(2):
+            cols = slice(h * HALF, (h + 1) * HALF)
+            nc.scalar.activation(log_rest[:, :, cols], ea[:, :, cols], ACT.Ln, bias=0.25)
+            for t in range(PACK):
+                nc.vector.scalar_tensor_tensor(
+                    logit[:, t, cols], a_bank[t][:, cols], tau_t[:, t : t + 1], log_rest[:, t, cols], ALU.mult, ALU.subtract
+                )
+        share = keep.tile([P, PACK, S], F32, name="share")
+        z_dealt = keep.tile([P, PACK, PACK, P], BF16, name="z_dealt")
+        for t in range(PACK):
+            nc.scalar.activation(share[:, t, :], logit[:, t, :], ACT.Sigmoid, bias=shift[t][:])
+            nc.vector.scalar_tensor_tensor(
+                z_dealt[:, :, t, :].rearrange("p u m -> p m u"),
+                a_bank[t][:].rearrange("p (m u) -> p m u", u=PACK), gt2[:, t : t + 1],
+                share[:, t, :].rearrange("p (m u) -> p m u", u=PACK), ALU.mult, ALU.mult,
+            )
+        old_rest = keep.tile([P, PACK - 1, S], F32, name="old_rest", tag="logit_then_old")
+        old = [old0[:]]
+        for u in range(1, PACK):
+            nc.scalar.activation(old_rest[:, u - 1, :], page[u][:].indirect(n2_t[:]), ACT.Copy)
+            old.append(old_rest[:, u - 1, :])
+
+        z_woven = [keep.tile([P, P, PACK], BF16, name=f"z_woven{u}", align_bytes=64) for u in range(PACK)]
+        cv_bank = []
+        for pair in range(2):
+            for u in (2 * pair, 2 * pair + 1):
+                weave(nc.vector.tensor_copy, z_woven[u][:], z_dealt[:, u, :, :])
+            for u in (2 * pair, 2 * pair + 1):
+                z_words, z_scales = quantize(z_woven[u][:], P, f"z_{u}")
+                bank = psum.tile([P, S], F32, name=f"cv_bank{u}", tag=f"late{u}")
+                nc.tensor.matmul_mx(
+                    out=bank[:], lhsT=z_words[:].bitcast(FP8X4), lhsT_scale=z_scales[:],
+                    rhs=z2_words[:].bitcast(FP8X4), rhs_scale=z2_scales[:], start=True, stop=True,
+                )
+                cv_bank.append(bank)
+        sg = []
+        for u in range(PACK):
+            cv_row = keep.tile([P, S], F32, name=f"cv_row{u}")
+            nc.vector.tensor_scalar(cv_row[:], cv_bank[u][:], 0.0625, None, ALU.mult)
+            gate = keep.tile([P, S], F32, name=f"sg{u}")
+            for h in range(2):
+                nc.scalar.activation(
+                    gate[:, h * HALF : (h + 1) * HALF], cv_row[:].indirect(n3_t[:, 16 * h : 16 * h + 16]), ACT.Sigmoid,
+                    bias=sg_bias[:, u : u + 1], scale=sl_t[:, u : u + 1],
+                )
+            sg.append(gate)
+        step = [keep.tile([P, S], F32, name=f"step{u}") for u in range(PACK)]
+        gated = [keep.tile([P, S], F32, name=f"gated{u}") for u in range(PACK)]
+        nw = [keep.tile([P, S], F32, name=f"nw{u}") for u in range(PACK)]
+        for u in range(PACK):
+            nc.vector.scalar_tensor_tensor(step[u][:], cv_bank[u][:], 0.0625, old[u], ALU.mult, ALU.subtract)
+        for pair in range(2):
+            for u in (2 * pair, 2 * pair + 1):
+                nc.vector.tensor_tensor(gated[u][:], sg[u][:], step[u][:], ALU.mult)
+            for u in (2 * pair, 2 * pair + 1):
+                nc.vector.tensor_tensor(nw[u][:], gated[u][:], old[u], ALU.add)
+
+        out_rows = out_0.rearrange("(p t) c -> t p c", t=PACK)
+        woven_out = [keep.tile([P, U // 2, PACK], BF16, name=f"woven_out{h}", align_bytes=64) for h in range(2)]
+
+        def scatter(u, lo, hi):
+            nc.scalar.activation(page[u][:].indirect(n2_t[:, lo // 16 : hi // 16]), nw[u][:, lo:hi], ACT.Copy)
+
+        def finish(u):
+            nc.sync.dma_start(out_rows[u], page[u][:])
+            for h in range(2):
+                nc.vector.tensor_copy(woven_out[h][:, :, u], page[u][:, h * (U // 2) : (h + 1) * (U // 2)])
+
+        scatter(0, 0, 128)
+        for u in range(PACK):
+            if u + 1 < PACK:
+                scatter(u + 1, 0, 128)
+            scatter(u, 128, 512)
+            finish(u)
+
+        out_scales = keep.tile([P, U], U8, name="out_scales", align_bytes=64)
+        word_rows = out_1[0].rearrange("p c r -> p (c r)").bitcast(I32)
+        for h in range(2):
+            cols = slice(h * (U // 2), (h + 1) * (U // 2))
+            out_words = keep.tile([P, U // 2], U32, name=f"out_words{h}", align_bytes=64)
+            nc.vector.quantize_mx(
+                out=out_words[:].bitcast(FP8X4), scales=out_scales[:, cols], in_=woven_out[h][:].rearrange("p w j -> p (w j)")
+            )
+            nc.sync.dma_start(word_rows[:, cols], out_words[:].bitcast(I32))
+        for q in range(4):
+            queue = nc.scalar if q % 2 == 0 else nc.sync
+            queue.dma_start(out_2[0][4 * q : 4 * q + 4, :].bitcast(I32), out_scales[32 * q : 32 * q + 4, :].bitcast(I32))

@@ -18,6 +18,7 @@ T = 2048
 S = 512
 U = 1024
 HALF = 256
+ORDER = (3, 0, 1, 2)
 FLOPS = 3 * 2 * 512 * 512 * 512
 
 
@@ -53,9 +54,11 @@ def tile_picked_momeshepg_none_po_kernel(
             return words, scales
 
         x_scale_table = keep.tile([P, T], U8, name="x_scale_table")
-        nc.vector.memset(x_scale_table[:].bitcast(I32), 0)
+        nc.vector.memset(x_scale_table[:, : T // 2].bitcast(I32), 0)
+        nc.gpsimd.memset(x_scale_table[:, T // 2 :].bitcast(I32), 0)
         offs_t = load_list(offs, "offs_t")
         two_t = load_list(two, "two_t")
+        n2_t = load_list(n2, "n2_t")
         for q in range(4):
             nc.sync.dma_start(x_scale_table[32 * q : 32 * q + 4, :].bitcast(I32), x_scales[0][4 * q : 4 * q + 4, :].bitcast(I32))
         x_word_table = keep.tile([P, T], U32, name="x_word_table")
@@ -68,19 +71,23 @@ def tile_picked_momeshepg_none_po_kernel(
             wa_raw.append(raw)
         mem_rows = mem.rearrange("(p t) c -> t p c", t=PACK)
         page = [keep.tile([P, U], F32, name=f"page{t}") for t in range(PACK)]
-        n2_t = load_list(n2, "n2_t")
         n1_t = load_list(n1, "n1_t")
         tau_t = load_rows(tau, "tau_t")
-        nc.sync.dma_start(page[0][:], mem_rows[0])
+        for u in ORDER[:2]:
+            nc.sync.dma_start(page[u][:], mem_rows[u])
         wb_raw = keep.tile([P, PACK, S], F32, name="wb_raw")
         nc.sync.dma_start(wb_raw[:], wb.rearrange("(p j) n -> p j n", j=PACK))
         gi_t = load_rows(gi, "gi_t")
         gt_t = load_rows(gt, "gt_t")
-        for t in range(1, PACK):
-            nc.sync.dma_start(page[t][:], mem_rows[t])
+        for u in ORDER[2:]:
+            nc.sync.dma_start(page[u][:], mem_rows[u])
         n3_t = load_list(n3, "n3_t")
         sl_t = load_rows(sl, "sl_t")
         th_t = load_rows(th, "th_t")
+
+        row = [keep.tile([P, 2 * S], F32, name=f"row{t}") for t in range(PACK)]
+        for t in range(PACK):
+            nc.gpsimd.memset(row[t][:, S:], 0.0)
 
         def pick(table, entries, dtype, name):
             picked = keep.tile([P, PACK, P], dtype, name=name, align_bytes=64)
@@ -106,28 +113,25 @@ def tile_picked_momeshepg_none_po_kernel(
                     rhs=wa_q[h][0][:].bitcast(FP8X4), rhs_scale=wa_q[h][1][:],
                     start=True, stop=True,
                 )
+        old_early = keep.tile([P, 2, S], F32, name="old_early")
+        old = {}
+        for i, u in enumerate(ORDER[:2]):
+            old[u] = old_early[:, i, :]
+            nc.scalar.activation(old[u], page[u][:].indirect(n2_t[:]), ACT.Copy)
         ea = keep.tile([P, PACK, S], F32, name="ea")
         shift = []
         for t in range(PACK):
-            a_row = keep.tile([P, S], F32, name=f"a_row{t}")
             top = keep.tile([P, 1], F32, name=f"top{t}")
-            nc.vector.tensor_scalar(a_row[:], a_bank[t][:], 1.0, None, ALU.mult, ALU.max, accum_out=top[:])
+            nc.vector.tensor_scalar(row[t][:, :S], a_bank[t][:], 1.0, None, ALU.mult, ALU.max, accum_out=top[:])
             bias = keep.tile([P, 1], F32, name=f"shift{t}")
             nc.gpsimd.tensor_scalar(bias[:], top[:], tau_t[:, t : t + 1], -1.0, ALU.mult, ALU.mult)
             shift.append(bias)
-            for h in range(2):
-                nc.scalar.activation(
-                    ea[:, t, h * HALF : (h + 1) * HALF], a_row[:].indirect(n1_t[:, 16 * h : 16 * h + 16]), ACT.Exp,
-                    bias=bias[:], scale=tau_t[:, t : t + 1],
-                )
-
-        old0 = keep.tile([P, S], F32, name="old0")
-        nc.scalar.activation(old0[:], page[0][:].indirect(n2_t[:]), ACT.Copy)
+            nc.scalar.activation(ea[:, t, :], row[t][:].indirect(n1_t[:]), ACT.Exp, bias=bias[:], scale=tau_t[:, t : t + 1])
 
         wb_woven = keep.tile([P, S, PACK], BF16, name="wb_woven", align_bytes=64)
         weave(nc.vector.tensor_copy, wb_woven[:], wb_raw[:])
         wb_words, wb_scales = quantize(wb_woven[:], S, "wb")
-        z2 = keep.tile([P, S, PACK], BF16, name="z2", align_bytes=64)
+        z2 = keep.tile([P, S, PACK], BF16, name="z2", tag="z2_logit_old", align_bytes=64)
         for c in range(4):
             b_bank = psum.tile([P, PACK, P], F32, name=f"b_bank{c}", tag=f"late{c}")
             for t in range(PACK):
@@ -148,7 +152,7 @@ def tile_picked_momeshepg_none_po_kernel(
         sg_bias = keep.tile([P, PACK], F32, name="sg_bias")
         nc.vector.scalar_tensor_tensor(sg_bias[:], sl_t[:], -1.0, th_t[:], ALU.mult, ALU.mult)
         log_rest = keep.tile([P, PACK, S], F32, name="log_rest")
-        logit = keep.tile([P, PACK, S], F32, name="logit", tag="logit_then_old")
+        logit = keep.tile([P, PACK, S], F32, name="logit", tag="z2_logit_old", align_bytes=64)
         for h in range(2):
             cols = slice(h * HALF, (h + 1) * HALF)
             nc.scalar.activation(log_rest[:, :, cols], ea[:, :, cols], ACT.Ln, bias=0.25)
@@ -158,81 +162,118 @@ def tile_picked_momeshepg_none_po_kernel(
                 )
         share = keep.tile([P, PACK, S], F32, name="share")
         z_dealt = keep.tile([P, PACK, PACK, P], BF16, name="z_dealt")
+        first, second, third, last = ORDER
+
+        def weigh(t, lo, hi):
+            nc.vector.scalar_tensor_tensor(
+                z_dealt[:, lo:hi, t, :].rearrange("p u m -> p m u"),
+                a_bank[t][:].rearrange("p (m u) -> p m u", u=PACK)[:, :, lo:hi], gt2[:, t : t + 1],
+                share[:, t, :].rearrange("p (m u) -> p m u", u=PACK)[:, :, lo:hi], ALU.mult, ALU.mult,
+            )
+
         for t in range(PACK):
             nc.scalar.activation(share[:, t, :], logit[:, t, :], ACT.Sigmoid, bias=shift[t][:])
-            nc.vector.scalar_tensor_tensor(
-                z_dealt[:, :, t, :].rearrange("p u m -> p m u"),
-                a_bank[t][:].rearrange("p (m u) -> p m u", u=PACK), gt2[:, t : t + 1],
-                share[:, t, :].rearrange("p (m u) -> p m u", u=PACK), ALU.mult, ALU.mult,
-            )
-        old_rest = keep.tile([P, PACK - 1, S], F32, name="old_rest", tag="logit_then_old")
-        old = [old0[:]]
-        for u in range(1, PACK):
-            nc.scalar.activation(old_rest[:, u - 1, :], page[u][:].indirect(n2_t[:]), ACT.Copy)
-            old.append(old_rest[:, u - 1, :])
+            if t < PACK - 1:
+                weigh(t, 0, PACK)
+        weigh(PACK - 1, first, first + 1)
+        old_late = keep.tile([P, 2, S], F32, name="old_late", tag="z2_logit_old", align_bytes=64)
+        for i, u in enumerate(ORDER[2:]):
+            old[u] = old_late[:, i, :]
+            nc.scalar.activation(old[u], page[u][:].indirect(n2_t[:]), ACT.Copy)
 
         z_woven = [keep.tile([P, P, PACK], BF16, name=f"z_woven{u}", align_bytes=64) for u in range(PACK)]
-        cv_bank = []
-        for pair in range(2):
-            for u in (2 * pair, 2 * pair + 1):
-                weave(nc.vector.tensor_copy, z_woven[u][:], z_dealt[:, u, :, :])
-            for u in (2 * pair, 2 * pair + 1):
-                z_words, z_scales = quantize(z_woven[u][:], P, f"z_{u}")
-                bank = psum.tile([P, S], F32, name=f"cv_bank{u}", tag=f"late{u}")
-                nc.tensor.matmul_mx(
-                    out=bank[:], lhsT=z_words[:].bitcast(FP8X4), lhsT_scale=z_scales[:],
-                    rhs=z2_words[:].bitcast(FP8X4), rhs_scale=z2_scales[:], start=True, stop=True,
-                )
-                cv_bank.append(bank)
-        sg = []
-        for u in range(PACK):
-            cv_row = keep.tile([P, S], F32, name=f"cv_row{u}")
-            nc.vector.tensor_scalar(cv_row[:], cv_bank[u][:], 0.0625, None, ALU.mult)
-            gate = keep.tile([P, S], F32, name=f"sg{u}")
-            for h in range(2):
-                nc.scalar.activation(
-                    gate[:, h * HALF : (h + 1) * HALF], cv_row[:].indirect(n3_t[:, 16 * h : 16 * h + 16]), ACT.Sigmoid,
-                    bias=sg_bias[:, u : u + 1], scale=sl_t[:, u : u + 1],
-                )
-            sg.append(gate)
+        cv_bank = {}
+        sg = [keep.tile([P, S], F32, name=f"sg{u}") for u in range(PACK)]
         step = [keep.tile([P, S], F32, name=f"step{u}") for u in range(PACK)]
         gated = [keep.tile([P, S], F32, name=f"gated{u}") for u in range(PACK)]
-        nw = [keep.tile([P, S], F32, name=f"nw{u}") for u in range(PACK)]
-        for u in range(PACK):
+        nw = {}
+
+        def weave_z(u):
+            weave(nc.vector.tensor_copy, z_woven[u][:], z_dealt[:, u, :, :])
+
+        def product(u):
+            z_words, z_scales = quantize(z_woven[u][:], P, f"z_{u}")
+            cv_bank[u] = psum.tile([P, S], F32, name=f"cv_bank{u}", tag=f"late{u}")
+            nc.tensor.matmul_mx(
+                out=cv_bank[u][:], lhsT=z_words[:].bitcast(FP8X4), lhsT_scale=z_scales[:],
+                rhs=z2_words[:].bitcast(FP8X4), rhs_scale=z2_scales[:], start=True, stop=True,
+            )
+
+        def gate(u):
+            nc.vector.tensor_scalar(row[u][:, :S], cv_bank[u][:], 0.0625, None, ALU.mult)
+            nc.scalar.activation(
+                sg[u][:], row[u][:].indirect(n3_t[:]), ACT.Sigmoid, bias=sg_bias[:, u : u + 1], scale=sl_t[:, u : u + 1]
+            )
+
+        def difference(u):
             nc.vector.scalar_tensor_tensor(step[u][:], cv_bank[u][:], 0.0625, old[u], ALU.mult, ALU.subtract)
-        for pair in range(2):
-            for u in (2 * pair, 2 * pair + 1):
-                nc.vector.tensor_tensor(gated[u][:], sg[u][:], step[u][:], ALU.mult)
-            for u in (2 * pair, 2 * pair + 1):
-                nc.vector.tensor_tensor(nw[u][:], gated[u][:], old[u], ALU.add)
+
+        def scale_step(u):
+            nc.vector.tensor_tensor(gated[u][:], sg[u][:], step[u][:], ALU.mult)
+
+        def add_old(u):
+            nw[u] = keep.tile([P, S], F32, name=f"nw{u}", tag=f"nw{min(u, 2)}")
+            nc.vector.tensor_tensor(nw[u][:], gated[u][:], old[u], ALU.add)
+
+        weave_z(first)
+        weigh(PACK - 1, 0, first)
+        product(first)
+        weave_z(second)
+        product(second)
+        weave_z(third)
+        gate(first)
+        weave_z(last)
+        gate(second)
+        product(third)
+        product(last)
+        difference(first)
+        gate(third)
+        scale_step(first)
+        gate(last)
+        add_old(first)
+        for u in (second, third):
+            difference(u)
+            scale_step(u)
+            add_old(u)
+        difference(last)
+        scale_step(last)
 
         out_rows = out_0.rearrange("(p t) c -> t p c", t=PACK)
-        woven_out = [keep.tile([P, U // 2, PACK], BF16, name=f"woven_out{h}", align_bytes=64) for h in range(2)]
+        parts = ((0, 512), (512, 768), (768, 1024))
+        woven_out = [keep.tile([P, hi - lo, PACK], BF16, name=f"woven_out{lo}", align_bytes=64) for lo, hi in parts]
 
         def scatter(u, lo, hi):
             nc.scalar.activation(page[u][:].indirect(n2_t[:, lo // 16 : hi // 16]), nw[u][:, lo:hi], ACT.Copy)
 
         def finish(u):
             nc.sync.dma_start(out_rows[u], page[u][:])
-            for h in range(2):
-                nc.vector.tensor_copy(woven_out[h][:, :, u], page[u][:, h * (U // 2) : (h + 1) * (U // 2)])
+            for i, (lo, hi) in enumerate(parts):
+                engine_copy = nc.scalar.copy if u == last and i > 0 else nc.vector.tensor_copy
+                engine_copy(woven_out[i][:, :, u], page[u][:, lo:hi])
 
-        scatter(0, 0, 128)
-        for u in range(PACK):
-            if u + 1 < PACK:
-                scatter(u + 1, 0, 128)
-            scatter(u, 128, 512)
-            finish(u)
+        scatter(first, 0, 384)
+        scatter(second, 0, 128)
+        scatter(first, 384, 512)
+        finish(first)
+        add_old(last)
+        scatter(second, 128, 512)
+        finish(second)
+        scatter(third, 0, 384)
+        scatter(last, 0, 128)
+        scatter(third, 384, 512)
+        finish(third)
+        scatter(last, 128, 512)
+        finish(last)
 
         out_scales = keep.tile([P, U], U8, name="out_scales", align_bytes=64)
         word_rows = out_1[0].rearrange("p c r -> p (c r)").bitcast(I32)
-        for h in range(2):
-            cols = slice(h * (U // 2), (h + 1) * (U // 2))
-            out_words = keep.tile([P, U // 2], U32, name=f"out_words{h}", align_bytes=64)
+        for i in (1, 0, 2):
+            lo, hi = parts[i]
+            out_words = keep.tile([P, hi - lo], U32, name=f"out_words{lo}", align_bytes=64)
             nc.vector.quantize_mx(
-                out=out_words[:].bitcast(FP8X4), scales=out_scales[:, cols], in_=woven_out[h][:].rearrange("p w j -> p (w j)")
+                out=out_words[:].bitcast(FP8X4), scales=out_scales[:, lo:hi], in_=woven_out[i][:].rearrange("p w j -> p (w j)")
             )
-            nc.sync.dma_start(word_rows[:, cols], out_words[:].bitcast(I32))
+            nc.sync.dma_start(word_rows[:, lo:hi], out_words[:].bitcast(I32))
         for q in range(4):
             queue = nc.scalar if q % 2 == 0 else nc.sync
             queue.dma_start(out_2[0][4 * q : 4 * q + 4, :].bitcast(I32), out_scales[32 * q : 32 * q + 4, :].bitcast(I32))

@@ -87,17 +87,27 @@ def tile_picked_momeshepg_none_po_kernel(
 
         row = [keep.tile([P, 2 * S], F32, name=f"row{t}") for t in range(PACK)]
         for t in range(PACK):
-            nc.gpsimd.memset(row[t][:, S:], 0.0)
+            nc.vector.memset(row[t][:, S:], 0.0)
 
         def pick(table, entries, dtype, name):
-            picked = keep.tile([P, PACK, P], dtype, name=name, align_bytes=64)
-            nc.vector.tensor_copy(picked[:].rearrange("p t m -> p m t"), table[:].indirect(entries[:]))
+            picked = keep.tile([P, S], dtype, name=name + "_picked")
+            nc.vector.tensor_copy(picked[:], table[:].indirect(entries[:]))
             return picked
 
-        xa_scales = pick(x_scale_table, offs_t, U8, "xa_scales")
-        xb_scales = pick(x_scale_table, two_t, U8, "xb_scales")
-        xa_words = pick(x_word_table, offs_t, U32, "xa_words")
-        xb_words = pick(x_word_table, two_t, U32, "xb_words")
+        def deal(picked, dtype, run, name):
+            dealt = keep.tile([P, PACK, P], dtype, name=name, align_bytes=64)
+            nc.vector.tensor_copy(
+                dealt[:].rearrange("p t (c i) -> p c t i", i=run),
+                picked[:].rearrange("p (c i t) -> p c t i", i=run, t=PACK),
+            )
+            return dealt
+
+        xa_scales_picked = pick(x_scale_table, offs_t, U8, "xa_scales")
+        xb_scales_picked = pick(x_scale_table, two_t, U8, "xb_scales")
+        xa_scales = deal(xa_scales_picked, U8, 16, "xa_scales")
+        xa_words_picked = pick(x_word_table, offs_t, U32, "xa_words")
+        xb_scales = deal(xb_scales_picked, U8, 16, "xb_scales")
+        xa_words = deal(xa_words_picked, U32, 4, "xa_words")
 
         a_bank = [psum.tile([P, S], F32, name=f"a_bank{t}") for t in range(PACK)]
         wa_q = []
@@ -105,6 +115,7 @@ def tile_picked_momeshepg_none_po_kernel(
             woven = keep.tile([P, HALF, PACK], BF16, name=f"wa_woven{h}", align_bytes=64)
             weave(nc.scalar.copy, woven[:], wa_raw[h][:])
             wa_q.append(quantize(woven[:], HALF, f"wa{h}"))
+        xb_words_picked = pick(x_word_table, two_t, U32, "xb_words")
         for h in range(2):
             for t in range(PACK):
                 nc.tensor.matmul_mx(
@@ -128,6 +139,7 @@ def tile_picked_momeshepg_none_po_kernel(
             shift.append(bias)
             nc.scalar.activation(ea[:, t, :], row[t][:].indirect(n1_t[:]), ACT.Exp, bias=bias[:], scale=tau_t[:, t : t + 1])
 
+        xb_words = deal(xb_words_picked, U32, 4, "xb_words")
         wb_woven = keep.tile([P, S, PACK], BF16, name="wb_woven", align_bytes=64)
         weave(nc.vector.tensor_copy, wb_woven[:], wb_raw[:])
         wb_words, wb_scales = quantize(wb_woven[:], S, "wb")
@@ -161,21 +173,14 @@ def tile_picked_momeshepg_none_po_kernel(
                     logit[:, t, cols], a_bank[t][:, cols], tau_t[:, t : t + 1], log_rest[:, t, cols], ALU.mult, ALU.subtract
                 )
         share = keep.tile([P, PACK, S], F32, name="share")
-        z_dealt = keep.tile([P, PACK, PACK, P], BF16, name="z_dealt")
+        z = keep.tile([P, PACK, S], BF16, name="z")
         first, second, third, last = ORDER
-
-        def weigh(t, lo, hi):
-            nc.vector.scalar_tensor_tensor(
-                z_dealt[:, lo:hi, t, :].rearrange("p u m -> p m u"),
-                a_bank[t][:].rearrange("p (m u) -> p m u", u=PACK)[:, :, lo:hi], gt2[:, t : t + 1],
-                share[:, t, :].rearrange("p (m u) -> p m u", u=PACK)[:, :, lo:hi], ALU.mult, ALU.mult,
-            )
 
         for t in range(PACK):
             nc.scalar.activation(share[:, t, :], logit[:, t, :], ACT.Sigmoid, bias=shift[t][:])
-            if t < PACK - 1:
-                weigh(t, 0, PACK)
-        weigh(PACK - 1, first, first + 1)
+            nc.vector.scalar_tensor_tensor(
+                z[:, t, :], a_bank[t][:], gt2[:, t : t + 1], share[:, t, :], ALU.mult, ALU.mult
+            )
         old_late = keep.tile([P, 2, S], F32, name="old_late", tag="z2_logit_old", align_bytes=64)
         for i, u in enumerate(ORDER[2:]):
             old[u] = old_late[:, i, :]
@@ -189,7 +194,10 @@ def tile_picked_momeshepg_none_po_kernel(
         nw = {}
 
         def weave_z(u):
-            weave(nc.vector.tensor_copy, z_woven[u][:], z_dealt[:, u, :, :])
+            nc.vector.tensor_copy(
+                z_woven[u][:].rearrange("p (c i) t -> p c t i", i=2),
+                z[:].rearrange("p t (c i u) -> p u c t i", i=2, u=PACK)[:, u],
+            )
 
         def product(u):
             z_words, z_scales = quantize(z_woven[u][:], P, f"z_{u}")
@@ -216,9 +224,8 @@ def tile_picked_momeshepg_none_po_kernel(
             nc.vector.tensor_tensor(nw[u][:], gated[u][:], old[u], ALU.add)
 
         weave_z(first)
-        weigh(PACK - 1, 0, first)
-        product(first)
         weave_z(second)
+        product(first)
         product(second)
         weave_z(third)
         gate(first)

@@ -89,33 +89,33 @@ def tile_picked_momeshepg_none_po_kernel(
         for t in range(PACK):
             nc.vector.memset(row[t][:, S:], 0.0)
 
-        def pick(table, entries, dtype, name):
-            picked = keep.tile([P, S], dtype, name=name + "_picked")
+        def pick(table, entries, dtype, name, tag):
+            picked = keep.tile([P, S], dtype, name=name + "_picked", tag=tag, align_bytes=64)
             nc.vector.tensor_copy(picked[:], table[:].indirect(entries[:]))
             return picked
 
-        def deal(picked, dtype, run, name):
-            dealt = keep.tile([P, PACK, P], dtype, name=name, align_bytes=64)
+        def deal(picked, dtype, run, name, tag):
+            dealt = keep.tile([P, PACK, P], dtype, name=name, tag=tag, align_bytes=64)
             nc.vector.tensor_copy(
                 dealt[:].rearrange("p t (c i) -> p c t i", i=run),
                 picked[:].rearrange("p (c i t) -> p c t i", i=run, t=PACK),
             )
             return dealt
 
-        xa_scales_picked = pick(x_scale_table, offs_t, U8, "xa_scales")
-        xb_scales_picked = pick(x_scale_table, two_t, U8, "xb_scales")
-        xa_scales = deal(xa_scales_picked, U8, 16, "xa_scales")
-        xa_words_picked = pick(x_word_table, offs_t, U32, "xa_words")
-        xb_scales = deal(xb_scales_picked, U8, 16, "xb_scales")
-        xa_words = deal(xa_words_picked, U32, 4, "xa_words")
+        xa_scales_picked = pick(x_scale_table, offs_t, U8, "xa_scales", "xa_scales_picked")
+        xb_scales_picked = pick(x_scale_table, two_t, U8, "xb_scales", "xb_scales_picked")
+        xa_scales = deal(xa_scales_picked, U8, 16, "xa_scales", "xa_scales")
+        xa_words_picked = pick(x_word_table, offs_t, U32, "xa_words", "xa_words_picked")
+        xb_scales = deal(xb_scales_picked, U8, 16, "xb_scales", "xb_scales")
+        xa_words = deal(xa_words_picked, U32, 4, "xa_words", "xa_words")
 
         a_bank = [psum.tile([P, S], F32, name=f"a_bank{t}") for t in range(PACK)]
         wa_q = []
         for h in range(2):
-            woven = keep.tile([P, HALF, PACK], BF16, name=f"wa_woven{h}", align_bytes=64)
+            woven = keep.tile([P, HALF, PACK], BF16, name=f"wa_woven{h}", tag=f"wa_slot{h}", align_bytes=64)
             weave(nc.scalar.copy, woven[:], wa_raw[h][:])
             wa_q.append(quantize(woven[:], HALF, f"wa{h}"))
-        xb_words_picked = pick(x_word_table, two_t, U32, "xb_words")
+        xb_words_picked = pick(x_word_table, two_t, U32, "xb_words", "wa_slot0")
         for h in range(2):
             for t in range(PACK):
                 nc.tensor.matmul_mx(
@@ -135,22 +135,26 @@ def tile_picked_momeshepg_none_po_kernel(
             top = keep.tile([P, 1], F32, name=f"top{t}")
             nc.vector.tensor_scalar(row[t][:, :S], a_bank[t][:], 1.0, None, ALU.mult, ALU.max, accum_out=top[:])
             bias = keep.tile([P, 1], F32, name=f"shift{t}")
-            nc.gpsimd.tensor_scalar(bias[:], top[:], tau_t[:, t : t + 1], -1.0, ALU.mult, ALU.mult)
+            engine = nc.gpsimd if t == 0 else nc.vector
+            engine.tensor_scalar(bias[:], top[:], tau_t[:, t : t + 1], -1.0, ALU.mult, ALU.mult)
             shift.append(bias)
             nc.scalar.activation(ea[:, t, :], row[t][:].indirect(n1_t[:]), ACT.Exp, bias=bias[:], scale=tau_t[:, t : t + 1])
 
-        xb_words = deal(xb_words_picked, U32, 4, "xb_words")
-        wb_woven = keep.tile([P, S, PACK], BF16, name="wb_woven", align_bytes=64)
-        weave(nc.vector.tensor_copy, wb_woven[:], wb_raw[:])
-        wb_words, wb_scales = quantize(wb_woven[:], S, "wb")
+        xb_words = deal(xb_words_picked, U32, 4, "xb_words", "wa_slot1")
+        wb_woven = [keep.tile([P, HALF, PACK], BF16, name=f"wb_woven{h}", align_bytes=64) for h in range(2)]
+        for h in range(2):
+            weave(nc.vector.tensor_copy, wb_woven[h][:], wb_raw[:, :, h * HALF : (h + 1) * HALF])
+        wb_q = [quantize(wb_woven[h][:], HALF, f"wb{h}") for h in range(2)]
         z2 = keep.tile([P, S, PACK], BF16, name="z2", tag="z2_logit_old", align_bytes=64)
         for c in range(4):
             b_bank = psum.tile([P, PACK, P], F32, name=f"b_bank{c}", tag=f"late{c}")
+            wb_words, wb_scales = wb_q[c // 2]
+            cols = slice(c % 2 * P, (c % 2 + 1) * P)
             for t in range(PACK):
                 nc.tensor.matmul_mx(
                     out=b_bank[:, t, :],
                     lhsT=xb_words[:, t, :].bitcast(FP8X4), lhsT_scale=xb_scales[:, t, :],
-                    rhs=wb_words[:, c * P : (c + 1) * P].bitcast(FP8X4), rhs_scale=wb_scales[:, c * P : (c + 1) * P],
+                    rhs=wb_words[:, cols].bitcast(FP8X4), rhs_scale=wb_scales[:, cols],
                     start=True, stop=True,
                 )
             nc.vector.tensor_tensor(
@@ -160,9 +164,11 @@ def tile_picked_momeshepg_none_po_kernel(
         z2_words, z2_scales = quantize(z2[:], S, "z2")
 
         gt2 = keep.tile([P, PACK], F32, name="gt2")
-        nc.vector.tensor_scalar(gt2[:], gt_t[:], 2.0, None, ALU.mult)
+        nc.gpsimd.tensor_scalar(gt2[:], gt_t[:], 2.0, 0.0, ALU.mult, ALU.add)
+        neg_sl = keep.tile([P, PACK], F32, name="neg_sl")
+        nc.gpsimd.tensor_scalar(neg_sl[:], sl_t[:], -1.0, 0.0, ALU.mult, ALU.add)
         sg_bias = keep.tile([P, PACK], F32, name="sg_bias")
-        nc.vector.scalar_tensor_tensor(sg_bias[:], sl_t[:], -1.0, th_t[:], ALU.mult, ALU.mult)
+        nc.gpsimd.tensor_tensor(sg_bias[:], neg_sl[:], th_t[:], ALU.mult)
         log_rest = keep.tile([P, PACK, S], F32, name="log_rest")
         logit = keep.tile([P, PACK, S], F32, name="logit", tag="z2_logit_old", align_bytes=64)
         for h in range(2):

@@ -73,13 +73,13 @@ def tile_picked_momeshepg_none_po_kernel(
         page = [keep.tile([P, U], F32, name=f"page{t}") for t in range(PACK)]
         n1_t = load_list(n1, "n1_t")
         tau_t = load_rows(tau, "tau_t")
-        for u in ORDER[:2]:
+        for u in ORDER[:1]:
             nc.sync.dma_start(page[u][:], mem_rows[u])
         wb_raw = keep.tile([P, PACK, S], F32, name="wb_raw")
         nc.sync.dma_start(wb_raw[:], wb.rearrange("(p j) n -> p j n", j=PACK))
         gi_t = load_rows(gi, "gi_t")
         gt_t = load_rows(gt, "gt_t")
-        for u in ORDER[2:]:
+        for u in ORDER[1:]:
             nc.sync.dma_start(page[u][:], mem_rows[u])
         n3_t = load_list(n3, "n3_t")
         sl_t = load_rows(sl, "sl_t")
@@ -110,29 +110,33 @@ def tile_picked_momeshepg_none_po_kernel(
         xa_words = deal(xa_words_picked, U32, 4, "xa_words", "xa_words")
 
         a_bank = [psum.tile([P, S], F32, name=f"a_bank{t}") for t in range(PACK)]
-        wa_q = []
+        wa_words = keep.tile([P, S], U32, name="wa_words", align_bytes=64)
+        wa_scales = keep.tile([P, S], U8, name="wa_scales", align_bytes=64)
         for h in range(2):
-            woven = keep.tile([P, HALF, PACK], BF16, name=f"wa_woven{h}", tag=f"wa_slot{h}", align_bytes=64)
-            weave(nc.scalar.copy, woven[:], wa_raw[h][:])
-            wa_q.append(quantize(woven[:], HALF, f"wa{h}"))
-        xb_words_picked = pick(x_word_table, two_t, U32, "xb_words", "wa_slot0")
-        for h in range(2):
-            for t in range(PACK):
-                nc.tensor.matmul_mx(
-                    out=a_bank[t][:, h * HALF : (h + 1) * HALF],
-                    lhsT=xa_words[:, t, :].bitcast(FP8X4), lhsT_scale=xa_scales[:, t, :],
-                    rhs=wa_q[h][0][:].bitcast(FP8X4), rhs_scale=wa_q[h][1][:],
-                    start=True, stop=True,
-                )
-        old_early = keep.tile([P, 2, S], F32, name="old_early")
+            woven = keep.tile([P, HALF, PACK], BF16, name=f"wa_woven{h}", align_bytes=64)
+            if h == 0:
+                weave(nc.scalar.copy, woven[:], wa_raw[h][:])
+            else:
+                weave(nc.scalar.copy, woven[:, :P, :], wa_raw[h][:, :, :P])
+                weave(nc.vector.tensor_copy, woven[:, P:, :], wa_raw[h][:, :, P:])
+            cols = slice(h * HALF, (h + 1) * HALF)
+            nc.vector.quantize_mx(
+                out=wa_words[:, cols].bitcast(FP8X4), scales=wa_scales[:, cols], in_=woven[:].rearrange("p w j -> p (w j)")
+            )
+        for t in range(PACK):
+            nc.tensor.matmul_mx(
+                out=a_bank[t][:], lhsT=xa_words[:, t, :].bitcast(FP8X4), lhsT_scale=xa_scales[:, t, :],
+                rhs=wa_words[:].bitcast(FP8X4), rhs_scale=wa_scales[:], start=True, stop=True,
+            )
+        old_early = keep.tile([P, 1, S], F32, name="old_early")
         old = {}
-        for i, u in enumerate(ORDER[:2]):
+        for i, u in enumerate(ORDER[:1]):
             old[u] = old_early[:, i, :]
             nc.scalar.activation(old[u], page[u][:].indirect(n2_t[:]), ACT.Copy)
         ea = keep.tile([P, PACK, S], F32, name="ea")
         shift = []
         for t in range(PACK):
-            top = keep.tile([P, 1], F32, name=f"top{t}")
+            top = keep.tile([P, 1], F32, name=f"top{t}", tag=f"top_slot{t}", align_bytes=64)
             nc.vector.tensor_scalar(row[t][:, :S], a_bank[t][:], 1.0, None, ALU.mult, ALU.max, accum_out=top[:])
             bias = keep.tile([P, 1], F32, name=f"shift{t}")
             engine = nc.gpsimd if t == 0 else nc.vector
@@ -140,10 +144,17 @@ def tile_picked_momeshepg_none_po_kernel(
             shift.append(bias)
             nc.scalar.activation(ea[:, t, :], row[t][:].indirect(n1_t[:]), ACT.Exp, bias=bias[:], scale=tau_t[:, t : t + 1])
 
-        xb_words = deal(xb_words_picked, U32, 4, "xb_words", "wa_slot1")
-        wb_woven = [keep.tile([P, HALF, PACK], BF16, name=f"wb_woven{h}", align_bytes=64) for h in range(2)]
-        for h in range(2):
-            weave(nc.vector.tensor_copy, wb_woven[h][:], wb_raw[:, :, h * HALF : (h + 1) * HALF])
+        xb_words_picked = pick(x_word_table, two_t, U32, "xb_words", "top_slot3")
+        xb_words = deal(xb_words_picked, U32, 4, "xb_words", "xb_words")
+        wb_woven = [
+            keep.tile([P, HALF, PACK], BF16, name="wb_woven0", align_bytes=64),
+            keep.tile([P, HALF, PACK], BF16, name="wb_woven1", tag="top_slot0", align_bytes=64),
+        ]
+        weave(nc.vector.tensor_copy, wb_woven[0][:], wb_raw[:, :, :HALF])
+        nc.gpsimd.tensor_scalar(
+            wb_woven[1][:].rearrange("p (c i) j -> p c j i", i=4),
+            wb_raw[:, :, HALF:].rearrange("p j (c i) -> p c j i", i=4), 1.0, 0.0, ALU.mult, ALU.add,
+        )
         wb_q = [quantize(wb_woven[h][:], HALF, f"wb{h}") for h in range(2)]
         z2 = keep.tile([P, S, PACK], BF16, name="z2", tag="z2_logit_old", align_bytes=64)
         for c in range(4):
@@ -171,13 +182,11 @@ def tile_picked_momeshepg_none_po_kernel(
         nc.gpsimd.tensor_tensor(sg_bias[:], neg_sl[:], th_t[:], ALU.mult)
         log_rest = keep.tile([P, PACK, S], F32, name="log_rest")
         logit = keep.tile([P, PACK, S], F32, name="logit", tag="z2_logit_old", align_bytes=64)
-        for h in range(2):
-            cols = slice(h * HALF, (h + 1) * HALF)
-            nc.scalar.activation(log_rest[:, :, cols], ea[:, :, cols], ACT.Ln, bias=0.25)
-            for t in range(PACK):
-                nc.vector.scalar_tensor_tensor(
-                    logit[:, t, cols], a_bank[t][:, cols], tau_t[:, t : t + 1], log_rest[:, t, cols], ALU.mult, ALU.subtract
-                )
+        nc.scalar.activation(log_rest[:], ea[:], ACT.Ln, bias=0.25)
+        for t in range(PACK):
+            nc.vector.scalar_tensor_tensor(
+                logit[:, t, :], a_bank[t][:], tau_t[:, t : t + 1], log_rest[:, t, :], ALU.mult, ALU.subtract
+            )
         share = keep.tile([P, PACK, S], F32, name="share")
         z = keep.tile([P, PACK, S], BF16, name="z")
         first, second, third, last = ORDER
@@ -187,8 +196,8 @@ def tile_picked_momeshepg_none_po_kernel(
             nc.vector.scalar_tensor_tensor(
                 z[:, t, :], a_bank[t][:], gt2[:, t : t + 1], share[:, t, :], ALU.mult, ALU.mult
             )
-        old_late = keep.tile([P, 2, S], F32, name="old_late", tag="z2_logit_old", align_bytes=64)
-        for i, u in enumerate(ORDER[2:]):
+        old_late = keep.tile([P, 3, S], F32, name="old_late", tag="z2_logit_old", align_bytes=64)
+        for i, u in enumerate(ORDER[1:]):
             old[u] = old_late[:, i, :]
             nc.scalar.activation(old[u], page[u][:].indirect(n2_t[:]), ACT.Copy)
 

from contextlib import ExitStack

import concourse.mybir as mybir

F32 = mybir.dt.float32
BF16 = mybir.dt.bfloat16
I32 = mybir.dt.int32
U32 = mybir.dt.uint32
U16 = mybir.dt.uint16
U8 = mybir.dt.uint8
FP8X4 = mybir.dt.float8_e4m3fn_x4
ALU = mybir.AluOpType
ACT = mybir.ActivationFunctionType

P = 128
PACK = 4
T = 2048
S = 512
U = 1024
HALF = 256
ORDER = (3, 0, 1, 2)
FLOPS = 3 * 2 * 512 * 512 * 512


def tile_picked_momeshepg_none_po_kernel(
    tc, x_words, x_scales, wa, wb, tau, gt, gi, mem, sl, th, offs, two, n1, n2, n3, out_0, out_1, out_2
):
    nc = tc.nc
    with ExitStack() as ctx:
        lists = ctx.enter_context(tc.tile_pool(name="lists", bufs=1))
        keep = ctx.enter_context(tc.tile_pool(name="keep", bufs=1))
        psum = ctx.enter_context(tc.psum_pool(name="psum", bufs=1))

        def load_list(src, name):
            tile = lists.tile([P, S // 16], U16, name=name)
            nc.sync.dma_start(tile[:], src)
            return tile

        def load_rows(src, name):
            tile = keep.tile([P, PACK], F32, name=name)
            nc.sync.dma_start(tile[:], src.rearrange("(p t) o -> p (t o)", t=PACK))
            return tile

        def weave(engine_copy, dst, src):
            engine_copy(
                out=dst.rearrange("p (c i) j -> p c j i", i=4),
                in_=src.rearrange("p j (c i) -> p c j i", i=4),
            )

        def quantize(src, width, name):
            words = keep.tile([P, width], U32, name=name + "_words", align_bytes=64)
            scales = keep.tile([P, width], U8, name=name + "_scales", align_bytes=64)
            nc.vector.quantize_mx(out=words[:].bitcast(FP8X4), scales=scales[:], in_=src.rearrange("p w j -> p (w j)"))
            return words, scales

        x_scale_table = keep.tile([P, T], U8, name="x_scale_table")
        nc.vector.memset(x_scale_table[:, : T // 2].bitcast(I32), 0)
        nc.gpsimd.memset(x_scale_table[:, T // 2 :].bitcast(I32), 0)
        offs_t = load_list(offs, "offs_t")
        two_t = load_list(two, "two_t")
        n2_t = load_list(n2, "n2_t")
        for q in range(4):
            nc.sync.dma_start(x_scale_table[32 * q : 32 * q + 4, :].bitcast(I32), x_scales[0][4 * q : 4 * q + 4, :].bitcast(I32))
        x_word_table = keep.tile([P, T], U32, name="x_word_table")
        nc.sync.dma_start(x_word_table[:].bitcast(I32), x_words[0].rearrange("p c r -> p (c r)").bitcast(I32))
        wa_rows = wa.rearrange("(p j) n -> p j n", j=PACK)
        wa_raw = []
        for h in range(2):
            raw = keep.tile([P, PACK, HALF], F32, name=f"wa_raw{h}")
            nc.sync.dma_start(raw[:], wa_rows[:, :, h * HALF : (h + 1) * HALF])
            wa_raw.append(raw)
        mem_rows = mem.rearrange("(p t) c -> t p c", t=PACK)
        page = [keep.tile([P, U], F32, name=f"page{t}") for t in range(PACK)]
        n1_t = load_list(n1, "n1_t")
        tau_t = load_rows(tau, "tau_t")
        for u in ORDER[:1]:
            nc.sync.dma_start(page[u][:], mem_rows[u])
        wb_raw = keep.tile([P, PACK, S], F32, name="wb_raw")
        nc.sync.dma_start(wb_raw[:], wb.rearrange("(p j) n -> p j n", j=PACK))
        gi_t = load_rows(gi, "gi_t")
        gt_t = load_rows(gt, "gt_t")
        for u in ORDER[1:]:
            nc.sync.dma_start(page[u][:], mem_rows[u])
        n3_t = load_list(n3, "n3_t")
        sl_t = load_rows(sl, "sl_t")
        th_t = load_rows(th, "th_t")

        row = [keep.tile([P, 2 * S], F32, name=f"row{t}") for t in range(PACK)]
        for t in range(PACK):
            nc.vector.memset(row[t][:, S:], 0.0)

        def pick(table, entries, dtype, name, tag):
            picked = keep.tile([P, S], dtype, name=name + "_picked", tag=tag, align_bytes=64)
            nc.vector.tensor_copy(picked[:], table[:].indirect(entries[:]))
            return picked

        def deal(picked, dtype, run, name, tag):
            dealt = keep.tile([P, PACK, P], dtype, name=name, tag=tag, align_bytes=64)
            nc.vector.tensor_copy(
                dealt[:].rearrange("p t (c i) -> p c t i", i=run),
                picked[:].rearrange("p (c i t) -> p c t i", i=run, t=PACK),
            )
            return dealt

        xa_scales_picked = pick(x_scale_table, offs_t, U8, "xa_scales", "xa_scales_picked")
        xb_scales_picked = pick(x_scale_table, two_t, U8, "xb_scales", "xb_scales_picked")
        xa_scales = deal(xa_scales_picked, U8, 16, "xa_scales", "xa_scales")
        xa_words_picked = pick(x_word_table, offs_t, U32, "xa_words", "xa_words_picked")
        xb_scales = deal(xb_scales_picked, U8, 16, "xb_scales", "xb_scales")
        xa_words = deal(xa_words_picked, U32, 4, "xa_words", "xa_words")

        a_bank = [psum.tile([P, S], F32, name=f"a_bank{t}") for t in range(PACK)]
        wa_words = keep.tile([P, S], U32, name="wa_words", align_bytes=64)
        wa_scales = keep.tile([P, S], U8, name="wa_scales", align_bytes=64)
        for h in range(2):
            woven = keep.tile([P, HALF, PACK], BF16, name=f"wa_woven{h}", align_bytes=64)
            if h == 0:
                weave(nc.scalar.copy, woven[:], wa_raw[h][:])
            else:
                weave(nc.scalar.copy, woven[:, :P, :], wa_raw[h][:, :, :P])
                weave(nc.vector.tensor_copy, woven[:, P:, :], wa_raw[h][:, :, P:])
            cols = slice(h * HALF, (h + 1) * HALF)
            nc.vector.quantize_mx(
                out=wa_words[:, cols].bitcast(FP8X4), scales=wa_scales[:, cols], in_=woven[:].rearrange("p w j -> p (w j)")
            )
        for t in range(PACK):
            nc.tensor.matmul_mx(
                out=a_bank[t][:], lhsT=xa_words[:, t, :].bitcast(FP8X4), lhsT_scale=xa_scales[:, t, :],
                rhs=wa_words[:].bitcast(FP8X4), rhs_scale=wa_scales[:], start=True, stop=True,
            )
        old_early = keep.tile([P, 1, S], F32, name="old_early")
        old = {}
        for i, u in enumerate(ORDER[:1]):
            old[u] = old_early[:, i, :]
            nc.scalar.activation(old[u], page[u][:].indirect(n2_t[:]), ACT.Copy)
        ea = keep.tile([P, PACK, S], F32, name="ea")
        shift = []
        for t in range(PACK):
            top = keep.tile([P, 1], F32, name=f"top{t}", tag=f"top_slot{t}", align_bytes=64)
            nc.vector.tensor_scalar(row[t][:, :S], a_bank[t][:], 1.0, None, ALU.mult, ALU.max, accum_out=top[:])
            bias = keep.tile([P, 1], F32, name=f"shift{t}")
            engine = nc.gpsimd if t == 0 else nc.vector
            engine.tensor_scalar(bias[:], top[:], tau_t[:, t : t + 1], -1.0, ALU.mult, ALU.mult)
            shift.append(bias)
            nc.scalar.activation(ea[:, t, :], row[t][:].indirect(n1_t[:]), ACT.Exp, bias=bias[:], scale=tau_t[:, t : t + 1])

        xb_words_picked = pick(x_word_table, two_t, U32, "xb_words", "top_slot3")
        xb_words = deal(xb_words_picked, U32, 4, "xb_words", "xb_words")
        wb_woven = [
            keep.tile([P, HALF, PACK], BF16, name="wb_woven0", align_bytes=64),
            keep.tile([P, HALF, PACK], BF16, name="wb_woven1", tag="top_slot0", align_bytes=64),
        ]
        weave(nc.vector.tensor_copy, wb_woven[0][:], wb_raw[:, :, :HALF])
        nc.gpsimd.tensor_scalar(
            wb_woven[1][:].rearrange("p (c i) j -> p c j i", i=4),
            wb_raw[:, :, HALF:].rearrange("p j (c i) -> p c j i", i=4), 1.0, 0.0, ALU.mult, ALU.add,
        )
        wb_q = [quantize(wb_woven[h][:], HALF, f"wb{h}") for h in range(2)]
        z2 = keep.tile([P, S, PACK], BF16, name="z2", tag="z2_logit_old", align_bytes=64)
        for c in range(4):
            b_bank = psum.tile([P, PACK, P], F32, name=f"b_bank{c}", tag=f"late{c}")
            wb_words, wb_scales = wb_q[c // 2]
            cols = slice(c % 2 * P, (c % 2 + 1) * P)
            for t in range(PACK):
                nc.tensor.matmul_mx(
                    out=b_bank[:, t, :],
                    lhsT=xb_words[:, t, :].bitcast(FP8X4), lhsT_scale=xb_scales[:, t, :],
                    rhs=wb_words[:, cols].bitcast(FP8X4), rhs_scale=wb_scales[:, cols],
                    start=True, stop=True,
                )
            nc.vector.tensor_tensor(
                z2[:, c * P : (c + 1) * P, :], b_bank[:].rearrange("p t n -> p n t"),
                gi_t[:].unsqueeze(1).to_broadcast([P, P, PACK]), ALU.mult,
            )
        z2_words, z2_scales = quantize(z2[:], S, "z2")

        gt2 = keep.tile([P, PACK], F32, name="gt2")
        nc.gpsimd.tensor_scalar(gt2[:], gt_t[:], 2.0, 0.0, ALU.mult, ALU.add)
        neg_sl = keep.tile([P, PACK], F32, name="neg_sl")
        nc.gpsimd.tensor_scalar(neg_sl[:], sl_t[:], -1.0, 0.0, ALU.mult, ALU.add)
        sg_bias = keep.tile([P, PACK], F32, name="sg_bias")
        nc.gpsimd.tensor_tensor(sg_bias[:], neg_sl[:], th_t[:], ALU.mult)
        log_rest = keep.tile([P, PACK, S], F32, name="log_rest")
        logit = keep.tile([P, PACK, S], F32, name="logit", tag="z2_logit_old", align_bytes=64)
        nc.scalar.activation(log_rest[:], ea[:], ACT.Ln, bias=0.25)
        for t in range(PACK):
            nc.vector.scalar_tensor_tensor(
                logit[:, t, :], a_bank[t][:], tau_t[:, t : t + 1], log_rest[:, t, :], ALU.mult, ALU.subtract
            )
        share = keep.tile([P, PACK, S], F32, name="share")
        z = keep.tile([P, PACK, S], BF16, name="z")
        first, second, third, last = ORDER

        for t in range(PACK):
            nc.scalar.activation(share[:, t, :], logit[:, t, :], ACT.Sigmoid, bias=shift[t][:])
            nc.vector.scalar_tensor_tensor(
                z[:, t, :], a_bank[t][:], gt2[:, t : t + 1], share[:, t, :], ALU.mult, ALU.mult
            )
        old_late = keep.tile([P, 3, S], F32, name="old_late", tag="z2_logit_old", align_bytes=64)
        for i, u in enumerate(ORDER[1:]):
            old[u] = old_late[:, i, :]
            nc.scalar.activation(old[u], page[u][:].indirect(n2_t[:]), ACT.Copy)

        z_woven = [keep.tile([P, P, PACK], BF16, name=f"z_woven{u}", align_bytes=64) for u in range(PACK)]
        cv_bank = {}
        sg = [keep.tile([P, S], F32, name=f"sg{u}") for u in range(PACK)]
        step = [keep.tile([P, S], F32, name=f"step{u}") for u in range(PACK)]
        gated = [keep.tile([P, S], F32, name=f"gated{u}") for u in range(PACK)]
        nw = {}

        def weave_z(u):
            nc.vector.tensor_copy(
                z_woven[u][:].rearrange("p (c i) t -> p c t i", i=2),
                z[:].rearrange("p t (c i u) -> p u c t i", i=2, u=PACK)[:, u],
            )

        def product(u):
            z_words, z_scales = quantize(z_woven[u][:], P, f"z_{u}")
            cv_bank[u] = psum.tile([P, S], F32, name=f"cv_bank{u}", tag=f"late{u}")
            nc.tensor.matmul_mx(
                out=cv_bank[u][:], lhsT=z_words[:].bitcast(FP8X4), lhsT_scale=z_scales[:],
                rhs=z2_words[:].bitcast(FP8X4), rhs_scale=z2_scales[:], start=True, stop=True,
            )

        def gate(u):
            nc.vector.tensor_scalar(row[u][:, :S], cv_bank[u][:], 0.0625, None, ALU.mult)
            nc.scalar.activation(
                sg[u][:], row[u][:].indirect(n3_t[:]), ACT.Sigmoid, bias=sg_bias[:, u : u + 1], scale=sl_t[:, u : u + 1]
            )

        def difference(u):
            nc.vector.scalar_tensor_tensor(step[u][:], cv_bank[u][:], 0.0625, old[u], ALU.mult, ALU.subtract)

        def scale_step(u):
            nc.vector.tensor_tensor(gated[u][:], sg[u][:], step[u][:], ALU.mult)

        def add_old(u):
            nw[u] = keep.tile([P, S], F32, name=f"nw{u}", tag=f"nw{min(u, 2)}")
            nc.vector.tensor_tensor(nw[u][:], gated[u][:], old[u], ALU.add)

        weave_z(first)
        weave_z(second)
        product(first)
        product(second)
        weave_z(third)
        gate(first)
        weave_z(last)
        gate(second)
        product(third)
        product(last)
        difference(first)
        gate(third)
        scale_step(first)
        gate(last)
        add_old(first)
        for u in (second, third):
            difference(u)
            scale_step(u)
            add_old(u)
        difference(last)
        scale_step(last)

        out_rows = out_0.rearrange("(p t) c -> t p c", t=PACK)
        parts = ((0, 512), (512, 768), (768, 1024))
        woven_out = [keep.tile([P, hi - lo, PACK], BF16, name=f"woven_out{lo}", align_bytes=64) for lo, hi in parts]

        def scatter(u, lo, hi):
            nc.scalar.activation(page[u][:].indirect(n2_t[:, lo // 16 : hi // 16]), nw[u][:, lo:hi], ACT.Copy)

        def finish(u):
            nc.sync.dma_start(out_rows[u], page[u][:])
            for i, (lo, hi) in enumerate(parts):
                engine_copy = nc.scalar.copy if u == last and i > 0 else nc.vector.tensor_copy
                engine_copy(woven_out[i][:, :, u], page[u][:, lo:hi])

        scatter(first, 0, 384)
        scatter(second, 0, 128)
        scatter(first, 384, 512)
        finish(first)
        add_old(last)
        scatter(second, 128, 512)
        finish(second)
        scatter(third, 0, 384)
        scatter(last, 0, 128)
        scatter(third, 384, 512)
        finish(third)
        scatter(last, 128, 512)
        finish(last)

        out_scales = keep.tile([P, U], U8, name="out_scales", align_bytes=64)
        word_rows = out_1[0].rearrange("p c r -> p (c r)").bitcast(I32)
        for i in (1, 0, 2):
            lo, hi = parts[i]
            out_words = keep.tile([P, hi - lo], U32, name=f"out_words{lo}", align_bytes=64)
            nc.vector.quantize_mx(
                out=out_words[:].bitcast(FP8X4), scales=out_scales[:, lo:hi], in_=woven_out[i][:].rearrange("p w j -> p (w j)")
            )
            nc.sync.dma_start(word_rows[:, lo:hi], out_words[:].bitcast(I32))
        for q in range(4):
            queue = nc.scalar if q % 2 == 0 else nc.sync
            queue.dma_start(out_2[0][4 * q : 4 * q + 4, :].bitcast(I32), out_scales[32 * q : 32 * q + 4, :].bitcast(I32))
